import numpy as np
import ml_dtypes


def mxq(x, axis, fmt="e4m3"):
    dtype, down = {"e4m3": (ml_dtypes.float8_e4m3fn, 7), "e5m2": (ml_dtypes.float8_e5m2, 14)}[fmt]
    v = np.moveaxis(np.asarray(x, np.float32).astype(ml_dtypes.bfloat16).astype(np.float64), axis, -1)
    blocks = v.reshape(v.shape[:-1] + (-1, 32))
    amax = np.abs(blocks).max(-1, keepdims=True)
    byte = np.maximum(np.where(amax > 0, np.frexp(amax)[1] - 1 + 127, 0) - down, 1)
    scale = np.exp2(byte - 127.0)
    codes = (blocks / scale).astype(np.float32).astype(dtype).astype(np.float64)
    return np.moveaxis((codes * scale).reshape(v.shape), -1, axis)


WIDE = False


def mx_kscale(k):
    if not WIDE:
        return np.ones(k)
    levels = np.array([10, -10, 5, -5, 0])
    if k % 512:
        return np.exp2(np.random.permutation(np.resize(levels, k // 32))).repeat(32)
    a = np.empty((k // 512, 16))
    for p in range(k // 512):
        a[p, :8] = np.random.permutation(np.resize(levels, 8))
        for g in range(8):
            far = levels[np.abs(levels - a[p, g]) >= 10]
            a[p, g + 8] = far[np.random.randint(len(far))]
    return np.exp2(a.ravel()).repeat(32)


def f64(x):
    return np.asarray(x).astype(np.float64)


def striped(idx):
    return np.tile(np.asarray(idx).reshape(-1, 16).T, (8, 1)).astype(np.uint16)


def unstriped(offs):
    return offs[:16].T.reshape(-1).astype(np.int64)


E2M1 = np.array([0.0, 0.5, 1.0, 1.5, 2.0, 3.0, 4.0, 6.0, -0.0, -0.5, -1.0, -1.5, -2.0, -3.0, -4.0, -6.0])


def pack_weight(w, fmt):
    k, n = w.shape
    w = f64(np.asarray(w, np.float32).astype(ml_dtypes.bfloat16)).reshape(k // 32, 32, n)
    amax = np.abs(w).max(1)
    if fmt == "e4m3":
        byte = np.frexp(amax)[1] - 1 + 127 - 7
    else:
        mant, ex = np.frexp(amax / 6.0)
        byte = np.where(mant > 0.5, ex, ex - 1) + 127
    byte = np.clip(np.where(amax > 0, byte, 1), 1, 254)
    scaled = (w * np.exp2(127.0 - byte)[:, None, :]).reshape(k, n).astype(np.float32)
    by_word = np.ascontiguousarray(scaled.reshape(k // 512, 128, 4, n).transpose(0, 1, 3, 2))
    if fmt == "e4m3":
        words = by_word.astype(ml_dtypes.float8_e4m3fn).view(np.uint8)
    else:
        c = by_word.astype(ml_dtypes.float4_e2m1fn).view(np.uint8) & 0xF
        words = (c[..., 0::2] | (c[..., 1::2] << 4)).reshape(k // 512, 128, 2 * n)
    return np.ascontiguousarray(words), np.ascontiguousarray(byte.astype(np.uint8).reshape(k // 512, 16, n))


def unpack_weight(words, scales, fmt):
    g, _, n = scales.shape
    words = np.ascontiguousarray(words).reshape(g, 128, n, -1)
    if fmt == "e4m3":
        vals = words.view(ml_dtypes.float8_e4m3fn).astype(np.float64)
    else:
        nib = np.empty((g, 128, n, 4), np.uint8)
        nib[..., 0::2] = words & 0xF
        nib[..., 1::2] = words >> 4
        vals = E2M1[nib]
    vals = vals * np.repeat(np.exp2(scales.astype(np.float64) - 127.0), 8, axis=1)[..., None]
    return vals.transpose(0, 1, 3, 2).reshape(g * 512, n)


K, I, L, S, T, N = 1024, 512, 512, 512, 512, 512


def setup_inputs():
    n = np.random.standard_normal
    idx = np.random.randint(0, I, T)
    idx2 = np.random.randint(0, S, T)
    fk = mx_kscale(K)
    fl = mx_kscale(L)
    xap = pack_weight(n((K, I)) / fk[:, None], "e4m3")
    xbp = pack_weight(n((L, S)) / fl[:, None], "e2m1")
    wbp = pack_weight(n((L, N)) * 1 / np.sqrt(L) * fl[:, None], "e4m3")
    return {
        "xa_words": xap[0],
        "xa_scales": xap[1],
        "wa": (n((K, N)) * 1 / np.sqrt(K) * fk[:, None]).astype(np.float32),
        "xb_words": xbp[0],
        "xb_scales": xbp[1],
        "wb_words": wbp[0],
        "wb_scales": wbp[1],
        "ga": (np.random.uniform(0.3, 1.0, (1, T))).astype(np.float32),
        "gb": (np.random.uniform(0.3, 1.0, (1, T))).astype(np.float32),
        "offs": striped(idx),
        "offs2": striped(idx2),
    }


def reference(xa_words, xa_scales, wa, xb_words, xb_scales, wb_words, wb_scales, ga, gb, offs, offs2):
    idx = unstriped(offs)
    idx2 = unstriped(offs2)
    xau = unpack_weight(xa_words, xa_scales, "e4m3")
    xbu = unpack_weight(xb_words, xb_scales, "e2m1")
    wbu = unpack_weight(wb_words, wb_scales, "e4m3")
    waq = mxq(f64(wa), 0, "e4m3")
    za = waq.T @ xau
    zb = wbu.T @ xbu
    y = f64(ga) * za[:, idx] + f64(gb) * zb[:, idx2]
    return y

@@ -1,0 +1,168 @@
+from contextlib import ExitStack
+
+import concourse.mybir as mybir
+from concourse.masks import make_identity
+
+K, I, L, S, T, N = 1024, 512, 512, 512, 512, 512
+FLOPS = 2 * K * N * I + 2 * L * N * S
+
+F32 = mybir.dt.float32
+BF16 = mybir.dt.bfloat16
+I32 = mybir.dt.int32
+U32 = mybir.dt.uint32
+U16 = mybir.dt.uint16
+U8 = mybir.dt.uint8
+FP8X4 = mybir.dt.float8_e4m3fn_x4
+FP4X4 = mybir.dt.float4_e2m1fn_x4
+MULT = mybir.AluOpType.mult
+ADD = mybir.AluOpType.add
+
+P = 128
+PACK = 4
+PASSES = K // (P * PACK)
+TILES = N // P
+SPARE = 8
+
+
+def tile_list_combine_by_slot_number_kernel(tc, xa_words, xa_scales, wa, xb_words, xb_scales, wb_words, wb_scales, ga, gb, offs, offs2, out):
+    nc = tc.nc
+    with ExitStack() as ctx:
+        keep = ctx.enter_context(tc.tile_pool(name="keep", bufs=1))
+        psum = ctx.enter_context(tc.psum_pool(name="psum", bufs=1))
+
+        list_a = keep.tile([P, T // 16], U16)
+        list_b = keep.tile([P, T // 16], U16)
+        xb_codes = keep.tile([P, 2 * S], U8, align_bytes=64)
+        wb_codes = keep.tile([P, N], U32, align_bytes=64)
+        xa_codes = keep.tile([P, PASSES, I], U32, align_bytes=64)
+        b_planes = keep.tile([P, S + N], U8, align_bytes=64)
+        xa_plane = keep.tile([P, PASSES, I], U8, align_bytes=64)
+        ga_cols = keep.tile([P, PACK], F32)
+        gb_cols = keep.tile([P, PACK], F32)
+        ident = keep.tile([P, P], F32)
+
+        wa_raw = [keep.tile([P, PASSES, PACK, 2 * P], F32, name=f"wa_raw{h}") for h in range(2)]
+        wa_view = wa.rearrange("(z p t) n -> p z t n", z=PASSES, t=PACK)
+
+        def load_wa(h):
+            for z in range(PASSES):
+                nc.sync.dma_start(out=wa_raw[h][:, z], in_=wa_view[:, z, :, h * 2 * P : (h + 1) * 2 * P])
+
+        nc.gpsimd.memset(b_planes[:].bitcast(I32), 0)
+        make_identity(nc, ident[:])
+        nc.gpsimd.memset(xa_plane[:].rearrange("p z i -> p (z i)").bitcast(I32), 0)
+        nc.sync.dma_start(out=gb_cols[:], in_=gb[0].rearrange("(p c) -> p c", c=PACK))
+        nc.sync.dma_start(out=ga_cols[:], in_=ga[0].rearrange("(p c) -> p c", c=PACK))
+        nc.sync.dma_start(out=xb_codes[:].bitcast(I32), in_=xb_words[0].bitcast(I32))
+        nc.sync.dma_start(out=wb_codes[:].bitcast(I32), in_=wb_words[0].rearrange("p n t -> p (n t)").bitcast(I32))
+        for q in range(4):
+            nc.sync.dma_start(out=b_planes[32 * q : 32 * q + 4, 0:S].bitcast(I32), in_=xb_scales[0, 4 * q : 4 * q + 4, :].bitcast(I32))
+        for q in range(4):
+            nc.sync.dma_start(out=b_planes[32 * q : 32 * q + 4, S : S + N].bitcast(I32), in_=wb_scales[0, 4 * q : 4 * q + 4, :].bitcast(I32))
+        nc.sync.dma_start(list_b[:], offs2)
+        load_wa(0)
+        nc.sync.dma_start(out=xa_codes[:].bitcast(I32), in_=xa_words.rearrange("z p i t -> p z (i t)").bitcast(I32))
+        for q in range(4):
+            nc.sync.dma_start(
+                out=xa_plane[32 * q : 32 * q + 4, :, :].bitcast(I32),
+                in_=xa_scales[:, 4 * q : 4 * q + 4, :].rearrange("z r i -> r z i").bitcast(I32),
+            )
+        nc.sync.dma_start(list_a[:], offs)
+        load_wa(1)
+
+        za = [keep.tile([P, I + SPARE], F32, name=f"za{j}") for j in range(TILES)]
+        zb = [keep.tile([P, S + SPARE], F32, name=f"zb{j}") for j in range(TILES)]
+        for j in range(TILES):
+            nc.vector.memset(zb[j][:, S:], 0.0)
+        for j in range(TILES):
+            nc.vector.memset(za[j][:, I:], 0.0)
+
+        def spread(cols, name, tag):
+            bank = psum.tile([P, PACK, P], F32, name=name + "_bank", tag=tag)
+            for c in range(PACK):
+                nc.tensor.transpose(bank[:, c, :], cols[:, c : c + 1].to_broadcast([P, P]), ident[:])
+            rows = keep.tile([P, T], F32, name=name + "_rows")
+            nc.vector.tensor_copy(out=rows[:].rearrange("p (q c) -> p q c", c=PACK), in_=bank[:].rearrange("p c q -> p q c"))
+            return rows
+
+        gb_rows = spread(gb_cols, "gb", "b1")
+        ga_rows = spread(ga_cols, "ga", "b0")
+
+        picked_a = [keep.tile([P, T], F32, name=f"picked_a{j}") for j in range(TILES)]
+        picked_b = [keep.tile([P, T], F32, name=f"picked_b{j}") for j in range(TILES)]
+        grouped = [keep.tile([P, PASSES, P, PACK], BF16, name=f"grouped{j}", align_bytes=64) for j in range(TILES)]
+        codes = [keep.tile([P, PASSES * P], U32, name=f"wa_codes{j}", align_bytes=64) for j in range(TILES)]
+        plane = [keep.tile([P, PASSES * P], U8, name=f"wa_plane{j}", align_bytes=64) for j in range(TILES)]
+
+        def product_b(j):
+            bank = psum.tile([P, S], F32, name=f"zb_bank{j}", tag=f"b{j}")
+            nc.tensor.matmul_mx(
+                out=bank[:],
+                lhsT=wb_codes[:, j * P : (j + 1) * P].bitcast(FP8X4),
+                lhsT_scale=b_planes[:, S + j * P : S + (j + 1) * P],
+                rhs=xb_codes[:].bitcast(FP4X4),
+                rhs_scale=b_planes[:, 0:S],
+                start=True,
+                stop=True,
+            )
+            nc.scalar.copy(out=zb[j][:, 0:S], in_=bank[:])
+
+        def pick_b(j):
+            nc.vector.tensor_tensor(picked_b[j][:], zb[j][:].indirect(list_b[:]), gb_rows[:], MULT)
+
+        def round_wa(j):
+            nc.scalar.copy(out=grouped[j][:], in_=wa_raw[j // 2][:, :, :, (j % 2) * P : (j % 2 + 1) * P].rearrange("p z t n -> p z n t"))
+
+        def quantise_wa(j):
+            nc.vector.quantize_mx(out=codes[j][:].bitcast(FP8X4), scales=plane[j][:], in_=grouped[j][:].rearrange("p z n t -> p (z n t)"))
+
+        def product_a(j):
+            bank = psum.tile([P, I], F32, name=f"za_bank{j}")
+            for z in range(PASSES):
+                nc.tensor.matmul_mx(
+                    out=bank[:],
+                    lhsT=codes[j][:, z * P : (z + 1) * P].bitcast(FP8X4),
+                    lhsT_scale=plane[j][:, z * P : (z + 1) * P],
+                    rhs=xa_codes[:, z, :].bitcast(FP8X4),
+                    rhs_scale=xa_plane[:, z, :],
+                    start=(z == 0),
+                    stop=(z == PASSES - 1),
+                )
+            nc.scalar.copy(out=za[j][:, 0:I], in_=bank[:])
+
+        def pick_a(j):
+            nc.vector.tensor_tensor(picked_a[j][:], za[j][:].indirect(list_a[:]), ga_rows[:], MULT)
+
+        def finish(j):
+            y = keep.tile([P, T], F32, name=f"y{j}")
+            nc.vector.tensor_tensor(y[:], picked_a[j][:], picked_b[j][:], ADD)
+            nc.sync.dma_start(out=out[j * P : (j + 1) * P, :], in_=y[:])
+
+        product_b(0)
+        product_b(1)
+        pick_b(0)
+        round_wa(0)
+        pick_b(1)
+        quantise_wa(0)
+        product_b(2)
+        round_wa(1)
+        pick_b(2)
+        quantise_wa(1)
+        product_b(3)
+        product_a(0)
+        pick_b(3)
+        round_wa(2)
+        pick_a(0)
+        quantise_wa(2)
+        product_a(1)
+        finish(0)
+        round_wa(3)
+        pick_a(1)
+        quantise_wa(3)
+        product_a(2)
+        finish(1)
+        product_a(3)
+        pick_a(2)
+        pick_a(3)
+        finish(2)
+        finish(3)

@@ -41,24 +41,31 @@ def tile_list_combine_by_slot_number_kernel(tc, xa_words, xa_scales, wa, xb_word
         gb_cols = keep.tile([P, PACK], F32)
         ident = keep.tile([P, P], F32)
 
-        wa_raw = [keep.tile([P, PASSES, PACK, 2 * P], F32, name=f"wa_raw{h}") for h in range(2)]
+        chunks = [(0, 1), (1, 2), (2, 4)]
+        wa_raw = [keep.tile([P, PASSES, PACK, (hi - lo) * P], F32, name=f"wa_raw{lo}") for lo, hi in chunks]
         wa_view = wa.rearrange("(z p t) n -> p z t n", z=PASSES, t=PACK)
 
         def load_wa(h):
+            lo, hi = chunks[h]
             for z in range(PASSES):
-                nc.sync.dma_start(out=wa_raw[h][:, z], in_=wa_view[:, z, :, h * 2 * P : (h + 1) * 2 * P])
+                nc.sync.dma_start(out=wa_raw[h][:, z], in_=wa_view[:, z, :, lo * P : hi * P])
+
+        def load_plane(q, scales, lo):
+            nc.sync.dma_start(out=b_planes[32 * q : 32 * q + 4, lo : lo + S].bitcast(I32), in_=scales[0, 4 * q : 4 * q + 4, :].bitcast(I32))
 
         nc.gpsimd.memset(b_planes[:].bitcast(I32), 0)
         make_identity(nc, ident[:])
         nc.gpsimd.memset(xa_plane[:].rearrange("p z i -> p (z i)").bitcast(I32), 0)
         nc.sync.dma_start(out=gb_cols[:], in_=gb[0].rearrange("(p c) -> p c", c=PACK))
         nc.sync.dma_start(out=ga_cols[:], in_=ga[0].rearrange("(p c) -> p c", c=PACK))
+        load_plane(0, xb_scales, 0)
+        load_plane(1, xb_scales, 0)
         nc.sync.dma_start(out=xb_codes[:].bitcast(I32), in_=xb_words[0].bitcast(I32))
         nc.sync.dma_start(out=wb_codes[:].bitcast(I32), in_=wb_words[0].rearrange("p n t -> p (n t)").bitcast(I32))
+        load_plane(2, xb_scales, 0)
+        load_plane(3, xb_scales, 0)
         for q in range(4):
-            nc.sync.dma_start(out=b_planes[32 * q : 32 * q + 4, 0:S].bitcast(I32), in_=xb_scales[0, 4 * q : 4 * q + 4, :].bitcast(I32))
-        for q in range(4):
-            nc.sync.dma_start(out=b_planes[32 * q : 32 * q + 4, S : S + N].bitcast(I32), in_=wb_scales[0, 4 * q : 4 * q + 4, :].bitcast(I32))
+            load_plane(q, wb_scales, S)
         nc.sync.dma_start(list_b[:], offs2)
         load_wa(0)
         nc.sync.dma_start(out=xa_codes[:].bitcast(I32), in_=xa_words.rearrange("z p i t -> p z (i t)").bitcast(I32))
@@ -67,8 +74,9 @@ def tile_list_combine_by_slot_number_kernel(tc, xa_words, xa_scales, wa, xb_word
                 out=xa_plane[32 * q : 32 * q + 4, :, :].bitcast(I32),
                 in_=xa_scales[:, 4 * q : 4 * q + 4, :].rearrange("z r i -> r z i").bitcast(I32),
             )
-        nc.sync.dma_start(list_a[:], offs)
         load_wa(1)
+        load_wa(2)
+        nc.sync.dma_start(list_a[:], offs)
 
         za = [keep.tile([P, I + SPARE], F32, name=f"za{j}") for j in range(TILES)]
         zb = [keep.tile([P, S + SPARE], F32, name=f"zb{j}") for j in range(TILES)]
@@ -85,8 +93,8 @@ def tile_list_combine_by_slot_number_kernel(tc, xa_words, xa_scales, wa, xb_word
             nc.vector.tensor_copy(out=rows[:].rearrange("p (q c) -> p q c", c=PACK), in_=bank[:].rearrange("p c q -> p q c"))
             return rows
 
-        gb_rows = spread(gb_cols, "gb", "b1")
-        ga_rows = spread(ga_cols, "ga", "b0")
+        gb_rows = spread(gb_cols, "gb", "b0")
+        ga_rows = spread(ga_cols, "ga", "b1")
 
         picked_a = [keep.tile([P, T], F32, name=f"picked_a{j}") for j in range(TILES)]
         picked_b = [keep.tile([P, T], F32, name=f"picked_b{j}") for j in range(TILES)]
@@ -95,7 +103,7 @@ def tile_list_combine_by_slot_number_kernel(tc, xa_words, xa_scales, wa, xb_word
         plane = [keep.tile([P, PASSES * P], U8, name=f"wa_plane{j}", align_bytes=64) for j in range(TILES)]
 
         def product_b(j):
-            bank = psum.tile([P, S], F32, name=f"zb_bank{j}", tag=f"b{j}")
+            bank = psum.tile([P, S], F32, name=f"zb_bank{j}", tag=f"b{(j + 1) % 2}")
             nc.tensor.matmul_mx(
                 out=bank[:],
                 lhsT=wb_codes[:, j * P : (j + 1) * P].bitcast(FP8X4),
@@ -107,17 +115,67 @@ def tile_list_combine_by_slot_number_kernel(tc, xa_words, xa_scales, wa, xb_word
             )
             nc.scalar.copy(out=zb[j][:, 0:S], in_=bank[:])
 
+        def product_b_halves():
+            for h, tag in enumerate(("b0", "b1")):
+                cols = slice(h * S // 2, (h + 1) * S // 2)
+                bank = psum.tile([P, S // 2], F32, name=f"zb_half{h}", tag=tag)
+                nc.tensor.matmul_mx(
+                    out=bank[:],
+                    lhsT=wb_codes[:, 0:P].bitcast(FP8X4),
+                    lhsT_scale=b_planes[:, S : S + P],
+                    rhs=xb_codes[:, h * S : (h + 1) * S].bitcast(FP4X4),
+                    rhs_scale=b_planes[:, cols],
+                    start=True,
+                    stop=True,
+                )
+                if h == 0:
+                    nc.scalar.copy(out=zb[0][:, cols], in_=bank[:])
+                else:
+                    nc.vector.tensor_copy(out=zb[0][:, cols], in_=bank[:])
+
+        turned = {}
+
+        def turn(j, first):
+            if first:
+                turned[j] = psum.tile([P, TILES, P], F32, name=f"turned{j}")
+            src = picked_b[j] if first else picked_a[j]
+            for c in range(TILES):
+                nc.tensor.matmul(turned[j][:, c, :], lhsT=src[:, c * P : (c + 1) * P], rhs=ident[:], is_transpose=True,
+                                 start=(first and c == 0), stop=(not first and c == TILES - 1))
+
+        def turn_b(j):
+            turn(j, True)
+
+        def turn_a(j):
+            turn(j, False)
+            total = keep.tile([P, TILES, P], F32, name=f"total{j}")
+            nc.scalar.copy(out=total[:], in_=turned[j][:])
+            turned[j] = total
+
+        def turn_back(j):
+            bank = psum.tile([P, TILES, P], F32, name=f"back{j}")
+            for c in range(TILES):
+                nc.tensor.transpose(bank[:, c, :], turned[j][:, c, :], ident[:])
+            y = keep.tile([P, T], F32, name=f"y{j}")
+            nc.scalar.copy(out=y[:], in_=bank[:].rearrange("p c q -> p (c q)"))
+            nc.sync.dma_start(out=out[j * P : (j + 1) * P, :], in_=y[:])
+
         def pick_b(j):
             nc.vector.tensor_tensor(picked_b[j][:], zb[j][:].indirect(list_b[:]), gb_rows[:], MULT)
 
         def round_wa(j):
-            nc.scalar.copy(out=grouped[j][:], in_=wa_raw[j // 2][:, :, :, (j % 2) * P : (j % 2 + 1) * P].rearrange("p z t n -> p z n t"))
+            h = min(j, 2)
+            lo = (j - chunks[h][0]) * P
+            nc.scalar.copy(
+                out=grouped[j][:].rearrange("p z (c i) t -> p z c t i", i=PACK),
+                in_=wa_raw[h][:, :, :, lo : lo + P].rearrange("p z t (c i) -> p z c t i", i=PACK),
+            )
 
         def quantise_wa(j):
             nc.vector.quantize_mx(out=codes[j][:].bitcast(FP8X4), scales=plane[j][:], in_=grouped[j][:].rearrange("p z n t -> p (z n t)"))
 
         def product_a(j):
-            bank = psum.tile([P, I], F32, name=f"za_bank{j}")
+            bank = psum.tile([P, I], F32, name=f"za_bank{j}", tag=f"a{j % 2}")
             for z in range(PASSES):
                 nc.tensor.matmul_mx(
                     out=bank[:],
@@ -138,31 +196,50 @@ def tile_list_combine_by_slot_number_kernel(tc, xa_words, xa_scales, wa, xb_word
             nc.vector.tensor_tensor(y[:], picked_a[j][:], picked_b[j][:], ADD)
             nc.sync.dma_start(out=out[j * P : (j + 1) * P, :], in_=y[:])
 
-        product_b(0)
+        def pick_a_half(h):
+            cols = slice(h * T // 2, (h + 1) * T // 2)
+            j = TILES - 1
+            nc.vector.tensor_tensor(picked_a[j][:, cols], za[j][:].indirect(list_a[:, h * 16 : (h + 1) * 16]), ga_half[h], MULT)
+
+        def finish_half(h):
+            cols = slice(h * T // 2, (h + 1) * T // 2)
+            j = TILES - 1
+            y = keep.tile([P, T // 2], F32, name=f"y_half{h}")
+            nc.vector.tensor_tensor(y[:], picked_a[j][:, cols], picked_b[j][:, cols], ADD)
+            nc.sync.dma_start(out=out[j * P : (j + 1) * P, cols], in_=y[:])
+
+        ga_half = [ga_rows[:, 0 : T // 2], ga_rows[:, T // 2 : T]]
+        product_b_halves()
         product_b(1)
         pick_b(0)
         round_wa(0)
-        pick_b(1)
-        quantise_wa(0)
         product_b(2)
-        round_wa(1)
-        pick_b(2)
-        quantise_wa(1)
+        pick_b(1)
+        turn_b(0)
+        quantise_wa(0)
         product_b(3)
+        pick_b(2)
+        turn_b(1)
+        round_wa(1)
         product_a(0)
+        quantise_wa(1)
         pick_b(3)
         round_wa(2)
-        pick_a(0)
-        quantise_wa(2)
         product_a(1)
-        finish(0)
+        quantise_wa(2)
+        pick_a(0)
         round_wa(3)
-        pick_a(1)
-        quantise_wa(3)
         product_a(2)
-        finish(1)
+        turn_a(0)
+        quantise_wa(3)
+        pick_a(1)
+        turn_back(0)
         product_a(3)
         pick_a(2)
-        pick_a(3)
+        turn_a(1)
         finish(2)
-        finish(3)
+        turn_back(1)
+        pick_a_half(0)
+        pick_a_half(1)
+        finish_half(0)
+        finish_half(1)

from contextlib import ExitStack

import concourse.mybir as mybir
from concourse.masks import make_identity

K, I, L, S, T, N = 1024, 512, 512, 512, 512, 512
FLOPS = 2 * K * N * I + 2 * L * N * S

F32 = mybir.dt.float32
BF16 = mybir.dt.bfloat16
I32 = mybir.dt.int32
U32 = mybir.dt.uint32
U16 = mybir.dt.uint16
U8 = mybir.dt.uint8
FP8X4 = mybir.dt.float8_e4m3fn_x4
FP4X4 = mybir.dt.float4_e2m1fn_x4
MULT = mybir.AluOpType.mult
ADD = mybir.AluOpType.add

P = 128
PACK = 4
PASSES = K // (P * PACK)
TILES = N // P
SPARE = 8


def tile_list_combine_by_slot_number_kernel(tc, xa_words, xa_scales, wa, xb_words, xb_scales, wb_words, wb_scales, ga, gb, offs, offs2, out):
    nc = tc.nc
    with ExitStack() as ctx:
        keep = ctx.enter_context(tc.tile_pool(name="keep", bufs=1))
        psum = ctx.enter_context(tc.psum_pool(name="psum", bufs=1))

        list_a = keep.tile([P, T // 16], U16)
        list_b = keep.tile([P, T // 16], U16)
        xb_codes = keep.tile([P, 2 * S], U8, align_bytes=64)
        wb_codes = keep.tile([P, N], U32, align_bytes=64)
        xa_codes = keep.tile([P, PASSES, I], U32, align_bytes=64)
        b_planes = keep.tile([P, S + N], U8, align_bytes=64)
        xa_plane = keep.tile([P, PASSES, I], U8, align_bytes=64)
        ga_cols = keep.tile([P, PACK], F32)
        gb_cols = keep.tile([P, PACK], F32)
        ident = keep.tile([P, P], F32)

        chunks = [(0, 1), (1, 2), (2, 4)]
        wa_raw = [keep.tile([P, PASSES, PACK, (hi - lo) * P], F32, name=f"wa_raw{lo}") for lo, hi in chunks]
        wa_view = wa.rearrange("(z p t) n -> p z t n", z=PASSES, t=PACK)

        def load_wa(h):
            lo, hi = chunks[h]
            for z in range(PASSES):
                nc.sync.dma_start(out=wa_raw[h][:, z], in_=wa_view[:, z, :, lo * P : hi * P])

        def load_plane(q, scales, lo):
            nc.sync.dma_start(out=b_planes[32 * q : 32 * q + 4, lo : lo + S].bitcast(I32), in_=scales[0, 4 * q : 4 * q + 4, :].bitcast(I32))

        nc.gpsimd.memset(b_planes[:].bitcast(I32), 0)
        make_identity(nc, ident[:])
        nc.gpsimd.memset(xa_plane[:].rearrange("p z i -> p (z i)").bitcast(I32), 0)
        nc.sync.dma_start(out=gb_cols[:], in_=gb[0].rearrange("(p c) -> p c", c=PACK))
        nc.sync.dma_start(out=ga_cols[:], in_=ga[0].rearrange("(p c) -> p c", c=PACK))
        load_plane(0, xb_scales, 0)
        load_plane(1, xb_scales, 0)
        nc.sync.dma_start(out=xb_codes[:].bitcast(I32), in_=xb_words[0].bitcast(I32))
        nc.sync.dma_start(out=wb_codes[:].bitcast(I32), in_=wb_words[0].rearrange("p n t -> p (n t)").bitcast(I32))
        load_plane(2, xb_scales, 0)
        load_plane(3, xb_scales, 0)
        for q in range(4):
            load_plane(q, wb_scales, S)
        nc.sync.dma_start(list_b[:], offs2)
        load_wa(0)
        nc.sync.dma_start(out=xa_codes[:].bitcast(I32), in_=xa_words.rearrange("z p i t -> p z (i t)").bitcast(I32))
        for q in range(4):
            nc.sync.dma_start(
                out=xa_plane[32 * q : 32 * q + 4, :, :].bitcast(I32),
                in_=xa_scales[:, 4 * q : 4 * q + 4, :].rearrange("z r i -> r z i").bitcast(I32),
            )
        load_wa(1)
        load_wa(2)
        nc.sync.dma_start(list_a[:], offs)

        za = [keep.tile([P, I + SPARE], F32, name=f"za{j}") for j in range(TILES)]
        zb = [keep.tile([P, S + SPARE], F32, name=f"zb{j}") for j in range(TILES)]
        for j in range(TILES):
            nc.vector.memset(zb[j][:, S:], 0.0)
        for j in range(TILES):
            nc.vector.memset(za[j][:, I:], 0.0)

        def spread(cols, name, tag):
            bank = psum.tile([P, PACK, P], F32, name=name + "_bank", tag=tag)
            for c in range(PACK):
                nc.tensor.transpose(bank[:, c, :], cols[:, c : c + 1].to_broadcast([P, P]), ident[:])
            rows = keep.tile([P, T], F32, name=name + "_rows")
            nc.vector.tensor_copy(out=rows[:].rearrange("p (q c) -> p q c", c=PACK), in_=bank[:].rearrange("p c q -> p q c"))
            return rows

        gb_rows = spread(gb_cols, "gb", "b0")
        ga_rows = spread(ga_cols, "ga", "b1")

        picked_a = [keep.tile([P, T], F32, name=f"picked_a{j}") for j in range(TILES)]
        picked_b = [keep.tile([P, T], F32, name=f"picked_b{j}") for j in range(TILES)]
        grouped = [keep.tile([P, PASSES, P, PACK], BF16, name=f"grouped{j}", align_bytes=64) for j in range(TILES)]
        codes = [keep.tile([P, PASSES * P], U32, name=f"wa_codes{j}", align_bytes=64) for j in range(TILES)]
        plane = [keep.tile([P, PASSES * P], U8, name=f"wa_plane{j}", align_bytes=64) for j in range(TILES)]

        def product_b(j):
            bank = psum.tile([P, S], F32, name=f"zb_bank{j}", tag=f"b{(j + 1) % 2}")
            nc.tensor.matmul_mx(
                out=bank[:],
                lhsT=wb_codes[:, j * P : (j + 1) * P].bitcast(FP8X4),
                lhsT_scale=b_planes[:, S + j * P : S + (j + 1) * P],
                rhs=xb_codes[:].bitcast(FP4X4),
                rhs_scale=b_planes[:, 0:S],
                start=True,
                stop=True,
            )
            nc.scalar.copy(out=zb[j][:, 0:S], in_=bank[:])

        def product_b_halves():
            for h, tag in enumerate(("b0", "b1")):
                cols = slice(h * S // 2, (h + 1) * S // 2)
                bank = psum.tile([P, S // 2], F32, name=f"zb_half{h}", tag=tag)
                nc.tensor.matmul_mx(
                    out=bank[:],
                    lhsT=wb_codes[:, 0:P].bitcast(FP8X4),
                    lhsT_scale=b_planes[:, S : S + P],
                    rhs=xb_codes[:, h * S : (h + 1) * S].bitcast(FP4X4),
                    rhs_scale=b_planes[:, cols],
                    start=True,
                    stop=True,
                )
                if h == 0:
                    nc.scalar.copy(out=zb[0][:, cols], in_=bank[:])
                else:
                    nc.vector.tensor_copy(out=zb[0][:, cols], in_=bank[:])

        turned = {}

        def turn(j, first):
            if first:
                turned[j] = psum.tile([P, TILES, P], F32, name=f"turned{j}")
            src = picked_b[j] if first else picked_a[j]
            for c in range(TILES):
                nc.tensor.matmul(turned[j][:, c, :], lhsT=src[:, c * P : (c + 1) * P], rhs=ident[:], is_transpose=True,
                                 start=(first and c == 0), stop=(not first and c == TILES - 1))

        def turn_b(j):
            turn(j, True)

        def turn_a(j):
            turn(j, False)
            total = keep.tile([P, TILES, P], F32, name=f"total{j}")
            nc.scalar.copy(out=total[:], in_=turned[j][:])
            turned[j] = total

        def turn_back(j):
            bank = psum.tile([P, TILES, P], F32, name=f"back{j}")
            for c in range(TILES):
                nc.tensor.transpose(bank[:, c, :], turned[j][:, c, :], ident[:])
            y = keep.tile([P, T], F32, name=f"y{j}")
            nc.scalar.copy(out=y[:], in_=bank[:].rearrange("p c q -> p (c q)"))
            nc.sync.dma_start(out=out[j * P : (j + 1) * P, :], in_=y[:])

        def pick_b(j):
            nc.vector.tensor_tensor(picked_b[j][:], zb[j][:].indirect(list_b[:]), gb_rows[:], MULT)

        def round_wa(j):
            h = min(j, 2)
            lo = (j - chunks[h][0]) * P
            nc.scalar.copy(
                out=grouped[j][:].rearrange("p z (c i) t -> p z c t i", i=PACK),
                in_=wa_raw[h][:, :, :, lo : lo + P].rearrange("p z t (c i) -> p z c t i", i=PACK),
            )

        def quantise_wa(j):
            nc.vector.quantize_mx(out=codes[j][:].bitcast(FP8X4), scales=plane[j][:], in_=grouped[j][:].rearrange("p z n t -> p (z n t)"))

        def product_a(j):
            bank = psum.tile([P, I], F32, name=f"za_bank{j}", tag=f"a{j % 2}")
            for z in range(PASSES):
                nc.tensor.matmul_mx(
                    out=bank[:],
                    lhsT=codes[j][:, z * P : (z + 1) * P].bitcast(FP8X4),
                    lhsT_scale=plane[j][:, z * P : (z + 1) * P],
                    rhs=xa_codes[:, z, :].bitcast(FP8X4),
                    rhs_scale=xa_plane[:, z, :],
                    start=(z == 0),
                    stop=(z == PASSES - 1),
                )
            nc.scalar.copy(out=za[j][:, 0:I], in_=bank[:])

        def pick_a(j):
            nc.vector.tensor_tensor(picked_a[j][:], za[j][:].indirect(list_a[:]), ga_rows[:], MULT)

        def finish(j):
            y = keep.tile([P, T], F32, name=f"y{j}")
            nc.vector.tensor_tensor(y[:], picked_a[j][:], picked_b[j][:], ADD)
            nc.sync.dma_start(out=out[j * P : (j + 1) * P, :], in_=y[:])

        def pick_a_half(h):
            cols = slice(h * T // 2, (h + 1) * T // 2)
            j = TILES - 1
            nc.vector.tensor_tensor(picked_a[j][:, cols], za[j][:].indirect(list_a[:, h * 16 : (h + 1) * 16]), ga_half[h], MULT)

        def finish_half(h):
            cols = slice(h * T // 2, (h + 1) * T // 2)
            j = TILES - 1
            y = keep.tile([P, T // 2], F32, name=f"y_half{h}")
            nc.vector.tensor_tensor(y[:], picked_a[j][:, cols], picked_b[j][:, cols], ADD)
            nc.sync.dma_start(out=out[j * P : (j + 1) * P, cols], in_=y[:])

        ga_half = [ga_rows[:, 0 : T // 2], ga_rows[:, T // 2 : T]]
        product_b_halves()
        product_b(1)
        pick_b(0)
        round_wa(0)
        product_b(2)
        pick_b(1)
        turn_b(0)
        quantise_wa(0)
        product_b(3)
        pick_b(2)
        turn_b(1)
        round_wa(1)
        product_a(0)
        quantise_wa(1)
        pick_b(3)
        round_wa(2)
        product_a(1)
        quantise_wa(2)
        pick_a(0)
        round_wa(3)
        product_a(2)
        turn_a(0)
        quantise_wa(3)
        pick_a(1)
        turn_back(0)
        product_a(3)
        pick_a(2)
        turn_a(1)
        finish(2)
        turn_back(1)
        pick_a_half(0)
        pick_a_half(1)
        finish_half(0)
        finish_half(1)
